import numpy as np
import ml_dtypes


def mxq(x, axis, fmt="e4m3"):
    dtype, down = {"e4m3": (ml_dtypes.float8_e4m3fn, 7), "e5m2": (ml_dtypes.float8_e5m2, 14)}[fmt]
    v = np.moveaxis(np.asarray(x, np.float32).astype(ml_dtypes.bfloat16).astype(np.float64), axis, -1)
    blocks = v.reshape(v.shape[:-1] + (-1, 32))
    amax = np.abs(blocks).max(-1, keepdims=True)
    byte = np.maximum(np.where(amax > 0, np.frexp(amax)[1] - 1 + 127, 0) - down, 1)
    scale = np.exp2(byte - 127.0)
    codes = (blocks / scale).astype(np.float32).astype(dtype).astype(np.float64)
    return np.moveaxis((codes * scale).reshape(v.shape), -1, axis)


WIDE = False


def mx_kscale(k):
    if not WIDE:
        return np.ones(k)
    levels = np.array([10, -10, 5, -5, 0])
    if k % 512:
        return np.exp2(np.random.permutation(np.resize(levels, k // 32))).repeat(32)
    a = np.empty((k // 512, 16))
    for p in range(k // 512):
        a[p, :8] = np.random.permutation(np.resize(levels, 8))
        for g in range(8):
            far = levels[np.abs(levels - a[p, g]) >= 10]
            a[p, g + 8] = far[np.random.randint(len(far))]
    return np.exp2(a.ravel()).repeat(32)


def f64(x):
    return np.asarray(x).astype(np.float64)


def striped(idx):
    return np.tile(idx.reshape(-1, 16).T, (8, 1)).astype(np.uint16)


def unstriped(offs):
    return offs[:16].T.reshape(-1).astype(np.int64)


def striped8(idx):
    return np.concatenate([x.reshape(-1, 16).T for x in idx]).astype(np.uint16)


def runs(offs, k):
    lists = np.stack([offs[16 * r : 16 * r + 16].T.reshape(-1) for r in range(8)]).astype(np.int64)
    return lists[np.arange(k) % 512 // 64]


def pack_weight(w):
    k, n = w.shape
    w = f64(np.asarray(w, np.float32).astype(ml_dtypes.bfloat16)).reshape(k // 32, 32, n)
    amax = np.abs(w).max(1)
    byte = np.clip(np.where(amax > 0, np.frexp(amax)[1] - 1 + 127 - 7, 1), 1, 254)
    scaled = (w * np.exp2(127.0 - byte)[:, None, :]).reshape(k, n).astype(np.float32)
    words = np.ascontiguousarray(scaled.reshape(k // 512, 128, 4, n).transpose(0, 1, 3, 2)).astype(ml_dtypes.float8_e4m3fn).view(np.uint8)
    return words, np.ascontiguousarray(byte.astype(np.uint8).reshape(k // 512, 16, n))


def unpack_weight(words, scales):
    g, p, n, _ = words.shape
    vals = np.ascontiguousarray(words).view(ml_dtypes.float8_e4m3fn).astype(np.float64) * np.repeat(np.exp2(scales.astype(np.float64) - 127.0), 8, axis=1)[..., None]
    return vals.transpose(0, 1, 3, 2).reshape(g * 512, n)


K, T, S, G, H, W, C = 512, 1024, 512, 2048, 512, 256, 512


def setup_inputs():
    n = np.random.standard_normal
    s = mx_kscale(K)[:, None]
    packed_xT = pack_weight(n((K, T)) * s)
    packed_dT = pack_weight(n((K, G)) / s)
    perm = np.random.permutation(S)
    return {
        "x_words": packed_xT[0],
        "x_scales": packed_xT[1],
        "d_words": packed_dT[0],
        "d_scales": packed_dT[1],
        "gs": (np.random.uniform(0.5, 1.5, (K, 1)) / s).astype(np.float32),
        "offs": striped(np.random.permutation(T)[:S]),
        "k1": striped8(np.random.randint(0, G, (8, H))),
        "n1": striped(perm[:W]),
        "n2": striped(perm[W:]),
        "cand": striped(np.random.permutation(T)[:C]),
        "two": striped(np.random.permutation(T)[:S]),
        "k2": striped8(np.random.randint(0, G, (8, H))),
        "n3": striped8(np.stack([np.random.permutation(S) for _ in range(8)])),
        "n4": striped8(np.stack([np.random.permutation(S) for _ in range(8)])),
        "n5": striped8(np.stack([np.random.permutation(S) for _ in range(8)])),
    }


def reference(x_words, x_scales, d_words, d_scales, gs, offs, k1, n1, n2, cand, two, k2, n3, n4, n5):
    d_k2 = unpack_weight(d_words, d_scales)[np.arange(K)[:, None], runs(k2, K)]
    x_two = unpack_weight(x_words, x_scales)[:, unstriped(two)]
    b = 0.0625 * (d_k2.T @ x_two)
    x_cand = unpack_weight(x_words, x_scales)[:, unstriped(cand)]
    d_k1 = unpack_weight(d_words, d_scales)[np.arange(K)[:, None], runs(k1, K)]
    xq = unpack_weight(x_words, x_scales)[:, unstriped(offs)]
    h = 0.0625 * (d_k1.T @ xq)
    pa = h[:, unstriped(n1)]
    pb = h[:, unstriped(n2)]
    ra = np.maximum(pa, pb)
    ds = h.copy()
    ds[:, unstriped(n1)] = ra
    z = f64(gs) * ds
    a = 0.0625 * ((x_cand.T @ mxq(z, 0, "e4m3")))
    return b * (a[np.arange(C)[:, None], runs(n3, C)] - a) + 0.5 * ((b[np.arange(H)[:, None], runs(n5, H)]) * (a[np.arange(C)[:, None], runs(n4, C)] - a))

@@ -1,0 +1,245 @@
+from contextlib import ExitStack
+
+import concourse.mybir as mybir
+
+K, T, S, G, W = 512, 1024, 512, 2048, 256
+FLOPS = 3 * 2 * 512 * 512 * 512
+
+F32 = mybir.dt.float32
+BF16 = mybir.dt.bfloat16
+I32 = mybir.dt.int32
+U32 = mybir.dt.uint32
+U16 = mybir.dt.uint16
+U8 = mybir.dt.uint8
+FP8X4 = mybir.dt.float8_e4m3fn_x4
+ALU = mybir.AluOpType
+COPY = mybir.ActivationFunctionType.Copy
+
+P = 128
+NT = 4
+HALF = S // 2
+
+
+def tile_picked_pqcjflowbfill_none_p_kernel(
+    tc, x_words, x_scales, d_words, d_scales, gs, offs, k1, n1, n2, cand, two, k2, n3, n4, n5, out
+):
+    nc = tc.nc
+    with ExitStack() as ctx:
+        lists = ctx.enter_context(tc.tile_pool(name="lists", bufs=1))
+        keep = ctx.enter_context(tc.tile_pool(name="keep", bufs=1))
+        psum = ctx.enter_context(tc.psum_pool(name="psum", bufs=1))
+
+        def load_list(name, src):
+            tile = lists.tile(list(src.shape), U16, name=name)
+            nc.sync.dma_start(tile[:], src)
+            return tile
+
+        def sbuf(name, shape, dtype):
+            return keep.tile(shape, dtype, name=name, align_bytes=64)
+
+        k1_t = load_list("k1_t", k1)
+        d_sc = sbuf("d_sc", [P, G], U8)
+        d_rows = d_scales[0].bitcast(I32).rearrange("(g e) c -> e g c", e=2)
+        for e in range(2):
+            nc.sync.dma_start(
+                d_sc[:].bitcast(I32)[e:P:2, :], d_rows[e].unsqueeze(1).to_broadcast([8, 8, G // 4])
+            )
+        offs_t = load_list("offs_t", offs)
+        x_sc = sbuf("x_sc", [P, T], U8)
+        x_rows = x_scales[0].bitcast(I32)
+        for q in range(4):
+            nc.sync.dma_start(
+                x_sc[:].bitcast(I32)[32 * q : 32 * q + 32, :],
+                x_rows[4 * q : 4 * q + 4, :].unsqueeze(0).to_broadcast([8, 4, T // 4]),
+            )
+        x_w = sbuf("x_w", [P, T], I32)
+        nc.sync.dma_start(x_w[:], x_words[0].rearrange("p n t -> p (n t)").bitcast(I32))
+        d_w = sbuf("d_w", [P, G], I32)
+        nc.sync.dma_start(d_w[:], d_words[0].rearrange("p n t -> p (n t)").bitcast(I32))
+        k2_t = load_list("k2_t", k2)
+        n1_t = load_list("n1_t", n1)
+        n2_t = load_list("n2_t", n2)
+        two_t = load_list("two_t", two)
+        cand_t = load_list("cand_t", cand)
+        n5_t = load_list("n5_t", n5)
+        n3_t = load_list("n3_t", n3)
+        n4_t = load_list("n4_t", n4)
+        gs_t = sbuf("gs_t", [P, NT], F32)
+        nc.gpsimd.dma_start(gs_t[:], gs.rearrange("(p t) o -> p (t o)", t=NT))
+        gain = sbuf("gain", [P, NT], F32)
+        nc.scalar.activation(gain[:], gs_t[:], COPY, scale=0.0625)
+
+        def gather_codes(name, table, offsets, dtype):
+            tile = sbuf(name, [P, S], dtype)
+            nc.vector.tensor_copy(tile[:], table.indirect(offsets[:]))
+            return tile
+
+        def lift_odd_rows(plane, queue):
+            words = plane[:].bitcast(I32)
+            for e in range(2):
+                queue.dma_start(words[2 + e : P : 32, :], words[16 + e : P : 32, :])
+
+        x_w32 = x_w[:].bitcast(U32)
+        d_w32 = d_w[:].bitcast(U32)
+
+        k1_b = gather_codes("k1_b", d_sc[:], k1_t, U8)
+        w1_sc = sbuf("w1_sc", [P, S], U8)
+        nc.vector.tensor_copy(
+            w1_sc[:].rearrange("p (t m) -> p t m", t=NT), k1_b[:].rearrange("p (m t) -> p t m", t=NT)
+        )
+        lift_odd_rows(w1_sc, nc.scalar)
+        xq_sc = gather_codes("xq_sc", x_sc[:], offs_t, U8)
+        xq_w = gather_codes("xq_w", x_w32, offs_t, U32)
+        k1_w = gather_codes("k1_w", d_w32, k1_t, U32)
+        w1_w = sbuf("w1_w", [P, S], U32)
+        nc.vector.tensor_copy(
+            w1_w[:].rearrange("p (t c i) -> p c t i", t=NT, i=4),
+            k1_w[:].rearrange("p (c i t) -> p c t i", t=NT, i=4),
+        )
+
+        def product(tag, t, lhs_w, lhs_sc, rhs_w, rhs_sc):
+            bank = psum.tile([P, S], F32, name=tag + str(t), tag=tag + str(t))
+            cols = slice(P * t, P * t + P)
+            nc.tensor.matmul_mx(
+                out=bank[:],
+                lhsT=lhs_w[:, cols].bitcast(FP8X4),
+                lhsT_scale=lhs_sc[:, cols],
+                rhs=rhs_w[:].bitcast(FP8X4),
+                rhs_scale=rhs_sc[:],
+                start=True,
+                stop=True,
+            )
+            return bank
+
+        h_ps = [product("ha", t, w1_w, w1_sc, xq_w, xq_sc) for t in range(NT)]
+
+        def fetch(engine, dst, window, offsets):
+            if engine is nc.scalar:
+                nc.scalar.activation(dst, window.indirect(offsets), COPY)
+            else:
+                nc.vector.tensor_copy(dst, window.indirect(offsets))
+
+        h = [sbuf("h" + str(t), [P, S], F32) for t in range(NT)]
+        pa = [sbuf("pa" + str(t), [P, W], F32) for t in range(NT)]
+        pb = [sbuf("pb" + str(t), [P, W], F32) for t in range(NT)]
+        ra = [sbuf("ra" + str(t), [P, W], F32) for t in range(NT)]
+        z_pairs = sbuf("z_pairs", [P, 2 * S * 2], BF16)
+        z_pair = [z_pairs[:, 2 * S * u : 2 * S * (u + 1)].rearrange("p (j e) -> p j e", e=2) for u in range(2)]
+
+        def h_out(t):
+            nc.scalar.copy(h[t][:], h_ps[t][:])
+
+        def h_fetch(t, engine):
+            fetch(engine, pa[t][:], h[t][:], n1_t[:])
+            fetch(engine, pb[t][:], h[t][:], n2_t[:])
+
+        def h_max(t):
+            nc.vector.tensor_tensor(ra[t][:], pa[t][:], pb[t][:], ALU.max)
+
+        def h_put(t, engine):
+            if engine is nc.scalar:
+                nc.scalar.activation(h[t][:].indirect(n1_t[:]), ra[t][:], COPY)
+            else:
+                nc.vector.tensor_copy(h[t][:].indirect(n1_t[:]), ra[t][:])
+
+        def z_round(t, engine):
+            engine.tensor_scalar(
+                z_pair[t // 2][:, :, t % 2], h[t][:], gain[:, t : t + 1], 0.0, ALU.mult, ALU.add
+            )
+
+        def deal_bytes(name, src):
+            dst = sbuf(name, [P, S], U8)
+            nc.vector.tensor_copy(
+                dst[:].bitcast(I32).rearrange("p (t a w) -> p t a w", t=NT, w=2),
+                src[:].bitcast(I32).rearrange("p (a t w) -> p t a w", t=NT, w=2),
+            )
+            return dst
+
+        k2_b = gather_codes("k2_b", d_sc[:], k2_t, U8)
+        w2_sc = deal_bytes("w2_sc", k2_b)
+        lift_odd_rows(w2_sc, nc.sync)
+        k2_w = gather_codes("k2_w", d_w32, k2_t, U32)
+        w2_w = sbuf("w2_w", [P, S], U32)
+        nc.vector.tensor_copy(
+            w2_w[:].rearrange("p (t a b) -> p t a b", t=NT, b=8),
+            k2_w[:].rearrange("p (a t b) -> p t a b", t=NT, b=8),
+        )
+        for t in range(2):
+            h_out(t)
+            h_fetch(t, nc.scalar)
+            h_max(t)
+        x2_w = gather_codes("x2_w", x_w32, two_t, U32)
+        x2_sc = gather_codes("x2_sc", x_sc[:], two_t, U8)
+        b_ps = [product("b", t, w2_w, w2_sc, x2_w, x2_sc) for t in range(NT)]
+        h_out(2)
+        h_out(3)
+        h_fetch(2, nc.scalar)
+        h_max(2)
+        h_fetch(3, nc.vector)
+        h_max(3)
+        for t in range(3):
+            h_put(t, nc.scalar)
+        h_put(3, nc.vector)
+        z_round(0, nc.gpsimd)
+        z_round(1, nc.gpsimd)
+        xc_w = sbuf("xc_w", [P, S], U32)
+        nc.vector.tensor_copy(
+            xc_w[:].rearrange("p (t a b) -> p a t b", t=NT, b=8), x_w32.indirect(cand_t[:])
+        )
+        xc_b = gather_codes("xc_b", x_sc[:], cand_t, U8)
+        xc_sc = deal_bytes("xc_sc", xc_b)
+        z_round(2, nc.vector)
+        z_round(3, nc.vector)
+
+        z = sbuf("z", [P, S, 4], BF16)
+        nc.vector.tensor_copy(
+            z[:].rearrange("p j r -> p (j r)").bitcast(F32).rearrange("p (j u) -> p j u", u=2),
+            z_pairs[:].bitcast(F32).rearrange("p (u j) -> p j u", u=2),
+        )
+        z_w = sbuf("z_w", [P, S], U32)
+        z_sc = sbuf("z_sc", [P, S], U8)
+        nc.vector.quantize_mx(
+            out=z_w[:].bitcast(FP8X4), scales=z_sc[:], in_=z[:].rearrange("p j r -> p (j r)")
+        )
+        a_ps = [product("ha", t, xc_w, xc_sc, z_w, z_sc) for t in range(NT)]
+
+        def tiles(name):
+            return [sbuf(name + str(t), [P, S], F32) for t in range(NT)]
+
+        a_sb, b_sb, a3, a4, b5 = tiles("a_sb"), tiles("b_sb"), tiles("a3"), tiles("a4"), tiles("b5")
+        d3, d4, first, second, res = tiles("d3"), tiles("d4"), tiles("first"), tiles("second"), tiles("res")
+
+        def fetch8(engine, dst, window, offsets):
+            for u in range(2):
+                fetch(engine, dst[:, HALF * u : HALF * u + HALF], window[:], offsets[:, 16 * u : 16 * u + 16])
+
+        def b_fetch(t, engine):
+            if engine is nc.scalar:
+                nc.scalar.activation(b_sb[t][:], b_ps[t][:], COPY, scale=0.5 * 0.0625 * 0.0625)
+            else:
+                nc.vector.tensor_scalar(b_sb[t][:], b_ps[t][:], 0.5 * 0.0625 * 0.0625, None, ALU.mult)
+            fetch8(engine, b5[t], b_sb[t], n5_t)
+
+        out_rows = out.rearrange("(a t b) j -> t a b j", t=NT, b=8)
+
+        def finish(t):
+            nc.vector.tensor_tensor(d4[t][:], a4[t][:], a_ps[t][:], ALU.subtract)
+            nc.gpsimd.tensor_tensor(second[t][:], d4[t][:], b5[t][:], ALU.mult)
+            nc.vector.tensor_tensor(d3[t][:], a3[t][:], a_ps[t][:], ALU.subtract)
+            nc.vector.scalar_tensor_tensor(
+                first[t][:], d3[t][:], 0.0625 * 0.0625, b_ps[t][:], ALU.mult, ALU.mult
+            )
+            adder = nc.gpsimd if t < NT - 1 else nc.vector
+            adder.tensor_tensor(res[t][:], first[t][:], second[t][:], ALU.add)
+            nc.sync.dma_start(out_rows[t], res[t][:])
+
+        b_fetch(0, nc.scalar)
+        b_fetch(1, nc.scalar)
+        b_fetch(2, nc.vector)
+        for t in range(NT):
+            nc.scalar.copy(a_sb[t][:], a_ps[t][:])
+            fetch8(nc.vector if t < 3 else nc.scalar, a4[t], a_sb[t], n4_t)
+            fetch8(nc.scalar, a3[t], a_sb[t], n3_t)
+            if t == 2:
+                b_fetch(3, nc.scalar)
+            finish(t)

@@ -34,28 +34,23 @@ def tile_picked_pqcjflowbfill_none_p_kernel(
             nc.sync.dma_start(tile[:], src)
             return tile
 
-        def sbuf(name, shape, dtype):
-            return keep.tile(shape, dtype, name=name, align_bytes=64)
+        def sbuf(name, shape, dtype, tag=None):
+            return keep.tile(shape, dtype, name=name, tag=tag or name, align_bytes=64)
 
         k1_t = load_list("k1_t", k1)
         d_sc = sbuf("d_sc", [P, G], U8)
-        d_rows = d_scales[0].bitcast(I32).rearrange("(g e) c -> e g c", e=2)
-        for e in range(2):
-            nc.sync.dma_start(
-                d_sc[:].bitcast(I32)[e:P:2, :], d_rows[e].unsqueeze(1).to_broadcast([8, 8, G // 4])
-            )
+        nc.gpsimd.memset(d_sc[:].bitcast(I32), 0)
+        nc.sync.dma_start(d_sc[:].bitcast(I32)[0:P:8, :], d_scales[0].bitcast(I32))
         offs_t = load_list("offs_t", offs)
         x_sc = sbuf("x_sc", [P, T], U8)
         x_rows = x_scales[0].bitcast(I32)
+        nc.vector.memset(x_sc[:].bitcast(I32), 0)
         for q in range(4):
-            nc.sync.dma_start(
-                x_sc[:].bitcast(I32)[32 * q : 32 * q + 32, :],
-                x_rows[4 * q : 4 * q + 4, :].unsqueeze(0).to_broadcast([8, 4, T // 4]),
-            )
-        x_w = sbuf("x_w", [P, T], I32)
-        nc.sync.dma_start(x_w[:], x_words[0].rearrange("p n t -> p (n t)").bitcast(I32))
+            nc.sync.dma_start(x_sc[:].bitcast(I32)[32 * q : 32 * q + 4, :], x_rows[4 * q : 4 * q + 4, :])
         d_w = sbuf("d_w", [P, G], I32)
         nc.sync.dma_start(d_w[:], d_words[0].rearrange("p n t -> p (n t)").bitcast(I32))
+        x_w = sbuf("x_w", [P, T], I32)
+        nc.sync.dma_start(x_w[:], x_words[0].rearrange("p n t -> p (n t)").bitcast(I32))
         k2_t = load_list("k2_t", k2)
         n1_t = load_list("n1_t", n1)
         n2_t = load_list("n2_t", n2)
@@ -69,15 +64,15 @@ def tile_picked_pqcjflowbfill_none_p_kernel(
         gain = sbuf("gain", [P, NT], F32)
         nc.scalar.activation(gain[:], gs_t[:], COPY, scale=0.0625)
 
-        def gather_codes(name, table, offsets, dtype):
-            tile = sbuf(name, [P, S], dtype)
+        def gather_codes(name, table, offsets, dtype, tag=None):
+            tile = sbuf(name, [P, S], dtype, tag)
             nc.vector.tensor_copy(tile[:], table.indirect(offsets[:]))
             return tile
 
         def lift_odd_rows(plane, queue):
             words = plane[:].bitcast(I32)
-            for e in range(2):
-                queue.dma_start(words[2 + e : P : 32, :], words[16 + e : P : 32, :])
+            for c in range(1, 4):
+                queue.dma_start(words[c:P:32, :], words[8 * c : P : 32, :])
 
         x_w32 = x_w[:].bitcast(U32)
         d_w32 = d_w[:].bitcast(U32)
@@ -89,8 +84,8 @@ def tile_picked_pqcjflowbfill_none_p_kernel(
         )
         lift_odd_rows(w1_sc, nc.scalar)
         xq_sc = gather_codes("xq_sc", x_sc[:], offs_t, U8)
-        xq_w = gather_codes("xq_w", x_w32, offs_t, U32)
         k1_w = gather_codes("k1_w", d_w32, k1_t, U32)
+        xq_w = gather_codes("xq_w", x_w32, offs_t, U32)
         w1_w = sbuf("w1_w", [P, S], U32)
         nc.vector.tensor_copy(
             w1_w[:].rearrange("p (t c i) -> p c t i", t=NT, i=4),
@@ -142,7 +137,8 @@ def tile_picked_pqcjflowbfill_none_p_kernel(
             else:
                 nc.vector.tensor_copy(h[t][:].indirect(n1_t[:]), ra[t][:])
 
-        def z_round(t, engine):
+        def z_round(t):
+            engine = nc.gpsimd if t < 2 else nc.vector
             engine.tensor_scalar(
                 z_pair[t // 2][:, :, t % 2], h[t][:], gain[:, t : t + 1], 0.0, ALU.mult, ALU.add
             )
@@ -173,73 +169,126 @@ def tile_picked_pqcjflowbfill_none_p_kernel(
         b_ps = [product("b", t, w2_w, w2_sc, x2_w, x2_sc) for t in range(NT)]
         h_out(2)
         h_out(3)
+        fetch(nc.scalar, pa[3][:], h[3][:], n1_t[:])
+        fetch(nc.vector, pb[3][:], h[3][:], n2_t[:])
+        h_max(3)
         h_fetch(2, nc.scalar)
         h_max(2)
-        h_fetch(3, nc.vector)
-        h_max(3)
         for t in range(3):
             h_put(t, nc.scalar)
         h_put(3, nc.vector)
-        z_round(0, nc.gpsimd)
-        z_round(1, nc.gpsimd)
-        xc_w = sbuf("xc_w", [P, S], U32)
+        xc_w = sbuf("xc_w", [P, S], U32, tag="pa0")
         nc.vector.tensor_copy(
             xc_w[:].rearrange("p (t a b) -> p a t b", t=NT, b=8), x_w32.indirect(cand_t[:])
         )
-        xc_b = gather_codes("xc_b", x_sc[:], cand_t, U8)
+        xc_b = gather_codes("xc_b", x_sc[:], cand_t, U8, tag="pa1")
         xc_sc = deal_bytes("xc_sc", xc_b)
-        z_round(2, nc.vector)
-        z_round(3, nc.vector)
+        for t in (0, 3, 1, 2):
+            z_round(t)
 
-        z = sbuf("z", [P, S, 4], BF16)
-        nc.vector.tensor_copy(
-            z[:].rearrange("p j r -> p (j r)").bitcast(F32).rearrange("p (j u) -> p j u", u=2),
-            z_pairs[:].bitcast(F32).rearrange("p (u j) -> p j u", u=2),
-        )
+        z = sbuf("z", [P, S * 4], BF16)
         z_w = sbuf("z_w", [P, S], U32)
         z_sc = sbuf("z_sc", [P, S], U8)
-        nc.vector.quantize_mx(
-            out=z_w[:].bitcast(FP8X4), scales=z_sc[:], in_=z[:].rearrange("p j r -> p (j r)")
-        )
-        a_ps = [product("ha", t, xc_w, xc_sc, z_w, z_sc) for t in range(NT)]
+        halves = [slice(HALF * u, HALF * u + HALF) for u in range(2)]
+        for cols in halves:
+            nc.vector.tensor_copy(
+                z[:].bitcast(F32).rearrange("p (j u) -> p j u", u=2)[:, cols, :],
+                z_pairs[:].bitcast(F32).rearrange("p (u j) -> p j u", u=2)[:, cols, :],
+            )
+        for cols in halves:
+            nc.vector.quantize_mx(
+                out=z_w[:, cols].bitcast(FP8X4),
+                scales=z_sc[:, cols],
+                in_=z[:, 4 * cols.start : 4 * cols.stop],
+            )
+        a_ps = []
+        for t in range(NT):
+            bank = psum.tile([P, S], F32, name="ha" + str(t), tag="ha" + str(t))
+            rows = slice(P * t, P * t + P)
+            for cols in halves:
+                nc.tensor.matmul_mx(
+                    out=bank[:, cols],
+                    lhsT=xc_w[:, rows].bitcast(FP8X4),
+                    lhsT_scale=xc_sc[:, rows],
+                    rhs=z_w[:, cols].bitcast(FP8X4),
+                    rhs_scale=z_sc[:, cols],
+                    start=True,
+                    stop=True,
+                )
+            a_ps.append(bank)
 
         def tiles(name):
             return [sbuf(name + str(t), [P, S], F32) for t in range(NT)]
 
-        a_sb, b_sb, a3, a4, b5 = tiles("a_sb"), tiles("b_sb"), tiles("a3"), tiles("a4"), tiles("b5")
+        a3, a4, b5 = tiles("a3"), tiles("a4"), tiles("b5")
+        a_sb = [sbuf("a_sb" + str(t), [P, 2 * S], F32) for t in range(NT)]
         d3, d4, first, second, res = tiles("d3"), tiles("d4"), tiles("first"), tiles("second"), tiles("res")
+        b_sb = {}
 
         def fetch8(engine, dst, window, offsets):
-            for u in range(2):
-                fetch(engine, dst[:, HALF * u : HALF * u + HALF], window[:], offsets[:, 16 * u : 16 * u + 16])
+            fetch(engine, dst[:], window[:], offsets[:])
 
-        def b_fetch(t, engine):
+        def b_out(t, engine, tag):
+            b_sb[t] = sbuf("b_sb" + str(t), [P, 2 * S], F32, tag)
             if engine is nc.scalar:
-                nc.scalar.activation(b_sb[t][:], b_ps[t][:], COPY, scale=0.5 * 0.0625 * 0.0625)
+                nc.scalar.activation(b_sb[t][:, 0:S], b_ps[t][:], COPY, scale=0.5 * 0.0625 * 0.0625)
             else:
-                nc.vector.tensor_scalar(b_sb[t][:], b_ps[t][:], 0.5 * 0.0625 * 0.0625, None, ALU.mult)
-            fetch8(engine, b5[t], b_sb[t], n5_t)
+                nc.vector.tensor_scalar(b_sb[t][:, 0:S], b_ps[t][:], 0.5 * 0.0625 * 0.0625, None, ALU.mult)
+
+        def a_out(t, engine):
+            if engine is nc.scalar:
+                nc.scalar.copy(a_sb[t][:, 0:S], a_ps[t][:])
+            else:
+                nc.vector.tensor_copy(a_sb[t][:, 0:S], a_ps[t][:])
+
+        def a_fetch(t):
+            fetch8(nc.scalar, a4[t], a_sb[t], n4_t)
+            if t < NT - 1:
+                fetch8(nc.scalar, a3[t], a_sb[t], n3_t)
+            else:
+                for u in range(2):
+                    fetch(nc.scalar, a3[t][:, halves[u]], a_sb[t][:], n3_t[:, 16 * u : 16 * u + 16])
 
         out_rows = out.rearrange("(a t b) j -> t a b j", t=NT, b=8)
 
-        def finish(t):
-            nc.vector.tensor_tensor(d4[t][:], a4[t][:], a_ps[t][:], ALU.subtract)
+        def second_term(t):
+            if t == 0:
+                nc.gpsimd.tensor_tensor(d4[t][:], a4[t][:], a_sb[t][:, 0:S], ALU.subtract)
+            else:
+                nc.vector.tensor_tensor(d4[t][:], a4[t][:], a_ps[t][:], ALU.subtract)
             nc.gpsimd.tensor_tensor(second[t][:], d4[t][:], b5[t][:], ALU.mult)
-            nc.vector.tensor_tensor(d3[t][:], a3[t][:], a_ps[t][:], ALU.subtract)
-            nc.vector.scalar_tensor_tensor(
-                first[t][:], d3[t][:], 0.0625 * 0.0625, b_ps[t][:], ALU.mult, ALU.mult
-            )
-            adder = nc.gpsimd if t < NT - 1 else nc.vector
-            adder.tensor_tensor(res[t][:], first[t][:], second[t][:], ALU.add)
-            nc.sync.dma_start(out_rows[t], res[t][:])
 
-        b_fetch(0, nc.scalar)
-        b_fetch(1, nc.scalar)
-        b_fetch(2, nc.vector)
-        for t in range(NT):
-            nc.scalar.copy(a_sb[t][:], a_ps[t][:])
-            fetch8(nc.vector if t < 3 else nc.scalar, a4[t], a_sb[t], n4_t)
-            fetch8(nc.scalar, a3[t], a_sb[t], n3_t)
-            if t == 2:
-                b_fetch(3, nc.scalar)
-            finish(t)
+        def finish(t, cols, adder):
+            nc.vector.tensor_tensor(d3[t][:, cols], a3[t][:, cols], a_ps[t][:, cols], ALU.subtract)
+            nc.vector.scalar_tensor_tensor(
+                first[t][:, cols], d3[t][:, cols], 0.0625 * 0.0625, b_ps[t][:, cols], ALU.mult, ALU.mult
+            )
+            adder.tensor_tensor(res[t][:, cols], first[t][:, cols], second[t][:, cols], ALU.add)
+            nc.sync.dma_start(out_rows[t][:, :, cols], res[t][:, cols])
+
+        whole = slice(0, S)
+        b_out(0, nc.scalar, "ra1")
+        fetch8(nc.scalar, b5[0], b_sb[0], n5_t)
+        b_out(1, nc.scalar, "ra2")
+        a_out(0, nc.scalar)
+        a_fetch(0)
+        fetch8(nc.vector, b5[1], b_sb[1], n5_t)
+        a_out(1, nc.vector)
+        b_out(2, nc.vector, "z_pairs")
+        fetch8(nc.vector, b5[2], b_sb[2], n5_t)
+        a_fetch(1)
+        second_term(0)
+        finish(0, whole, nc.gpsimd)
+        a_out(2, nc.scalar)
+        a_fetch(2)
+        b_out(3, nc.vector, "a30")
+        second_term(1)
+        finish(1, whole, nc.gpsimd)
+        fetch8(nc.vector, b5[3], b_sb[3], n5_t)
+        a_out(3, nc.scalar)
+        a_fetch(3)
+        second_term(2)
+        second_term(3)
+        finish(2, whole, nc.gpsimd)
+        for cols in halves:
+            finish(3, cols, nc.vector)

@@ -138,9 +138,8 @@ def tile_picked_pqcjflowbfill_none_p_kernel(
                 nc.vector.tensor_copy(h[t][:].indirect(n1_t[:]), ra[t][:])
 
         def z_round(t):
-            engine = nc.gpsimd if t < 2 else nc.vector
-            engine.tensor_scalar(
-                z_pair[t // 2][:, :, t % 2], h[t][:], gain[:, t : t + 1], 0.0, ALU.mult, ALU.add
+            nc.vector.tensor_scalar(
+                z_pair[t // 2][:, :, t % 2], h[t][:], gain[:, t : t + 1], None, ALU.mult
             )
 
         def deal_bytes(name, src):
@@ -221,7 +220,7 @@ def tile_picked_pqcjflowbfill_none_p_kernel(
             return [sbuf(name + str(t), [P, S], F32) for t in range(NT)]
 
         a3, a4, b5 = tiles("a3"), tiles("a4"), tiles("b5")
-        a_sb = [sbuf("a_sb" + str(t), [P, 2 * S], F32) for t in range(NT)]
+        a_sb = {}
         d3, d4, first, second, res = tiles("d3"), tiles("d4"), tiles("first"), tiles("second"), tiles("res")
         b_sb = {}
 
@@ -235,60 +234,63 @@ def tile_picked_pqcjflowbfill_none_p_kernel(
             else:
                 nc.vector.tensor_scalar(b_sb[t][:, 0:S], b_ps[t][:], 0.5 * 0.0625 * 0.0625, None, ALU.mult)
 
-        def a_out(t, engine):
+        def a_out(t, engine, tag):
+            a_sb[t] = sbuf("a_sb" + str(t), [P, 2 * S], F32, tag)
             if engine is nc.scalar:
                 nc.scalar.copy(a_sb[t][:, 0:S], a_ps[t][:])
             else:
                 nc.vector.tensor_copy(a_sb[t][:, 0:S], a_ps[t][:])
 
-        def a_fetch(t):
-            fetch8(nc.scalar, a4[t], a_sb[t], n4_t)
-            if t < NT - 1:
-                fetch8(nc.scalar, a3[t], a_sb[t], n3_t)
-            else:
-                for u in range(2):
-                    fetch(nc.scalar, a3[t][:, halves[u]], a_sb[t][:], n3_t[:, 16 * u : 16 * u + 16])
-
         out_rows = out.rearrange("(a t b) j -> t a b j", t=NT, b=8)
 
-        def second_term(t):
+        def first_term(t):
+            nc.vector.tensor_tensor(d3[t][:], a3[t][:], a_ps[t][:], ALU.subtract)
+            nc.vector.scalar_tensor_tensor(
+                first[t][:], d3[t][:], 0.0625 * 0.0625, b_ps[t][:], ALU.mult, ALU.mult
+            )
+
+        def difference(t):
             if t == 0:
                 nc.gpsimd.tensor_tensor(d4[t][:], a4[t][:], a_sb[t][:, 0:S], ALU.subtract)
             else:
                 nc.vector.tensor_tensor(d4[t][:], a4[t][:], a_ps[t][:], ALU.subtract)
-            nc.gpsimd.tensor_tensor(second[t][:], d4[t][:], b5[t][:], ALU.mult)
 
-        def finish(t, cols, adder):
-            nc.vector.tensor_tensor(d3[t][:, cols], a3[t][:, cols], a_ps[t][:, cols], ALU.subtract)
-            nc.vector.scalar_tensor_tensor(
-                first[t][:, cols], d3[t][:, cols], 0.0625 * 0.0625, b_ps[t][:, cols], ALU.mult, ALU.mult
-            )
-            adder.tensor_tensor(res[t][:, cols], first[t][:, cols], second[t][:, cols], ALU.add)
+        def second_term(t, cols, engine):
+            engine.tensor_tensor(second[t][:, cols], d4[t][:, cols], b5[t][:, cols], ALU.mult)
+
+        def finish(t, cols, engine):
+            engine.tensor_tensor(res[t][:, cols], first[t][:, cols], second[t][:, cols], ALU.add)
             nc.sync.dma_start(out_rows[t][:, :, cols], res[t][:, cols])
+
+        def a_fetch(t):
+            fetch8(nc.scalar, a4[t], a_sb[t], n4_t)
+            fetch8(nc.scalar, a3[t], a_sb[t], n3_t)
 
         whole = slice(0, S)
         b_out(0, nc.scalar, "ra1")
         fetch8(nc.scalar, b5[0], b_sb[0], n5_t)
         b_out(1, nc.scalar, "ra2")
-        a_out(0, nc.scalar)
-        a_fetch(0)
+        a_out(0, nc.scalar, None)
         fetch8(nc.vector, b5[1], b_sb[1], n5_t)
-        a_out(1, nc.vector)
+        a_out(1, nc.vector, None)
         b_out(2, nc.vector, "z_pairs")
         fetch8(nc.vector, b5[2], b_sb[2], n5_t)
-        a_fetch(1)
-        second_term(0)
-        finish(0, whole, nc.gpsimd)
-        a_out(2, nc.scalar)
-        a_fetch(2)
-        b_out(3, nc.vector, "a30")
-        second_term(1)
-        finish(1, whole, nc.gpsimd)
-        fetch8(nc.vector, b5[3], b_sb[3], n5_t)
-        a_out(3, nc.scalar)
+        a_out(2, nc.vector, None)
+        for t in range(NT - 1):
+            a_fetch(t)
+            difference(t)
+            second_term(t, whole, nc.gpsimd)
+            first_term(t)
+            finish(t, whole, nc.gpsimd)
+            if t == 0:
+                a_out(3, nc.vector, "a30")
+            if t == 1:
+                b_out(3, nc.vector, "a31")
         a_fetch(3)
-        second_term(2)
-        second_term(3)
-        finish(2, whole, nc.gpsimd)
+        for u in range(2):
+            fetch(nc.scalar, b5[3][:, halves[u]], b_sb[3][:], n5_t[:, 16 * u : 16 * u + 16])
+        difference(3)
+        first_term(3)
         for cols in halves:
+            second_term(3, cols, nc.vector)
             finish(3, cols, nc.vector)

@@ -42,6 +42,8 @@ def tile_picked_pqcjflowbfill_none_p_kernel(
         nc.gpsimd.memset(d_sc[:].bitcast(I32), 0)
         nc.sync.dma_start(d_sc[:].bitcast(I32)[0:P:8, :], d_scales[0].bitcast(I32))
         offs_t = load_list("offs_t", offs)
+        x_w = sbuf("x_w", [P, T], I32)
+        nc.sync.dma_start(x_w[:], x_words[0].rearrange("p n t -> p (n t)").bitcast(I32))
         x_sc = sbuf("x_sc", [P, T], U8)
         x_rows = x_scales[0].bitcast(I32)
         nc.vector.memset(x_sc[:].bitcast(I32), 0)
@@ -49,16 +51,14 @@ def tile_picked_pqcjflowbfill_none_p_kernel(
             nc.sync.dma_start(x_sc[:].bitcast(I32)[32 * q : 32 * q + 4, :], x_rows[4 * q : 4 * q + 4, :])
         d_w = sbuf("d_w", [P, G], I32)
         nc.sync.dma_start(d_w[:], d_words[0].rearrange("p n t -> p (n t)").bitcast(I32))
-        x_w = sbuf("x_w", [P, T], I32)
-        nc.sync.dma_start(x_w[:], x_words[0].rearrange("p n t -> p (n t)").bitcast(I32))
         k2_t = load_list("k2_t", k2)
         n1_t = load_list("n1_t", n1)
         n2_t = load_list("n2_t", n2)
         two_t = load_list("two_t", two)
         cand_t = load_list("cand_t", cand)
         n5_t = load_list("n5_t", n5)
-        n3_t = load_list("n3_t", n3)
         n4_t = load_list("n4_t", n4)
+        n3_t = load_list("n3_t", n3)
         gs_t = sbuf("gs_t", [P, NT], F32)
         nc.gpsimd.dma_start(gs_t[:], gs.rearrange("(p t) o -> p (t o)", t=NT))
         gain = sbuf("gain", [P, NT], F32)
@@ -83,9 +83,9 @@ def tile_picked_pqcjflowbfill_none_p_kernel(
             w1_sc[:].rearrange("p (t m) -> p t m", t=NT), k1_b[:].rearrange("p (m t) -> p t m", t=NT)
         )
         lift_odd_rows(w1_sc, nc.scalar)
+        xq_w = gather_codes("xq_w", x_w32, offs_t, U32)
         xq_sc = gather_codes("xq_sc", x_sc[:], offs_t, U8)
         k1_w = gather_codes("k1_w", d_w32, k1_t, U32)
-        xq_w = gather_codes("xq_w", x_w32, offs_t, U32)
         w1_w = sbuf("w1_w", [P, S], U32)
         nc.vector.tensor_copy(
             w1_w[:].rearrange("p (t c i) -> p c t i", t=NT, i=4),
@@ -138,8 +138,9 @@ def tile_picked_pqcjflowbfill_none_p_kernel(
                 nc.vector.tensor_copy(h[t][:].indirect(n1_t[:]), ra[t][:])
 
         def z_round(t):
-            nc.vector.tensor_scalar(
-                z_pair[t // 2][:, :, t % 2], h[t][:], gain[:, t : t + 1], None, ALU.mult
+            engine = nc.gpsimd if t < 2 else nc.vector
+            engine.tensor_scalar(
+                z_pair[t // 2][:, :, t % 2], h[t][:], gain[:, t : t + 1], 0.0, ALU.mult, ALU.add
             )
 
         def deal_bytes(name, src):

from contextlib import ExitStack

import concourse.mybir as mybir

K, T, S, G, W = 512, 1024, 512, 2048, 256
FLOPS = 3 * 2 * 512 * 512 * 512

F32 = mybir.dt.float32
BF16 = mybir.dt.bfloat16
I32 = mybir.dt.int32
U32 = mybir.dt.uint32
U16 = mybir.dt.uint16
U8 = mybir.dt.uint8
FP8X4 = mybir.dt.float8_e4m3fn_x4
ALU = mybir.AluOpType
COPY = mybir.ActivationFunctionType.Copy

P = 128
NT = 4
HALF = S // 2


def tile_picked_pqcjflowbfill_none_p_kernel(
    tc, x_words, x_scales, d_words, d_scales, gs, offs, k1, n1, n2, cand, two, k2, n3, n4, n5, out
):
    nc = tc.nc
    with ExitStack() as ctx:
        lists = ctx.enter_context(tc.tile_pool(name="lists", bufs=1))
        keep = ctx.enter_context(tc.tile_pool(name="keep", bufs=1))
        psum = ctx.enter_context(tc.psum_pool(name="psum", bufs=1))

        def load_list(name, src):
            tile = lists.tile(list(src.shape), U16, name=name)
            nc.sync.dma_start(tile[:], src)
            return tile

        def sbuf(name, shape, dtype, tag=None):
            return keep.tile(shape, dtype, name=name, tag=tag or name, align_bytes=64)

        k1_t = load_list("k1_t", k1)
        d_sc = sbuf("d_sc", [P, G], U8)
        nc.gpsimd.memset(d_sc[:].bitcast(I32), 0)
        nc.sync.dma_start(d_sc[:].bitcast(I32)[0:P:8, :], d_scales[0].bitcast(I32))
        offs_t = load_list("offs_t", offs)
        x_w = sbuf("x_w", [P, T], I32)
        nc.sync.dma_start(x_w[:], x_words[0].rearrange("p n t -> p (n t)").bitcast(I32))
        x_sc = sbuf("x_sc", [P, T], U8)
        x_rows = x_scales[0].bitcast(I32)
        nc.vector.memset(x_sc[:].bitcast(I32), 0)
        for q in range(4):
            nc.sync.dma_start(x_sc[:].bitcast(I32)[32 * q : 32 * q + 4, :], x_rows[4 * q : 4 * q + 4, :])
        d_w = sbuf("d_w", [P, G], I32)
        nc.sync.dma_start(d_w[:], d_words[0].rearrange("p n t -> p (n t)").bitcast(I32))
        k2_t = load_list("k2_t", k2)
        n1_t = load_list("n1_t", n1)
        n2_t = load_list("n2_t", n2)
        two_t = load_list("two_t", two)
        cand_t = load_list("cand_t", cand)
        n5_t = load_list("n5_t", n5)
        n4_t = load_list("n4_t", n4)
        n3_t = load_list("n3_t", n3)
        gs_t = sbuf("gs_t", [P, NT], F32)
        nc.gpsimd.dma_start(gs_t[:], gs.rearrange("(p t) o -> p (t o)", t=NT))
        gain = sbuf("gain", [P, NT], F32)
        nc.scalar.activation(gain[:], gs_t[:], COPY, scale=0.0625)

        def gather_codes(name, table, offsets, dtype, tag=None):
            tile = sbuf(name, [P, S], dtype, tag)
            nc.vector.tensor_copy(tile[:], table.indirect(offsets[:]))
            return tile

        def lift_odd_rows(plane, queue):
            words = plane[:].bitcast(I32)
            for c in range(1, 4):
                queue.dma_start(words[c:P:32, :], words[8 * c : P : 32, :])

        x_w32 = x_w[:].bitcast(U32)
        d_w32 = d_w[:].bitcast(U32)

        k1_b = gather_codes("k1_b", d_sc[:], k1_t, U8)
        w1_sc = sbuf("w1_sc", [P, S], U8)
        nc.vector.tensor_copy(
            w1_sc[:].rearrange("p (t m) -> p t m", t=NT), k1_b[:].rearrange("p (m t) -> p t m", t=NT)
        )
        lift_odd_rows(w1_sc, nc.scalar)
        xq_w = gather_codes("xq_w", x_w32, offs_t, U32)
        xq_sc = gather_codes("xq_sc", x_sc[:], offs_t, U8)
        k1_w = gather_codes("k1_w", d_w32, k1_t, U32)
        w1_w = sbuf("w1_w", [P, S], U32)
        nc.vector.tensor_copy(
            w1_w[:].rearrange("p (t c i) -> p c t i", t=NT, i=4),
            k1_w[:].rearrange("p (c i t) -> p c t i", t=NT, i=4),
        )

        def product(tag, t, lhs_w, lhs_sc, rhs_w, rhs_sc):
            bank = psum.tile([P, S], F32, name=tag + str(t), tag=tag + str(t))
            cols = slice(P * t, P * t + P)
            nc.tensor.matmul_mx(
                out=bank[:],
                lhsT=lhs_w[:, cols].bitcast(FP8X4),
                lhsT_scale=lhs_sc[:, cols],
                rhs=rhs_w[:].bitcast(FP8X4),
                rhs_scale=rhs_sc[:],
                start=True,
                stop=True,
            )
            return bank

        h_ps = [product("ha", t, w1_w, w1_sc, xq_w, xq_sc) for t in range(NT)]

        def fetch(engine, dst, window, offsets):
            if engine is nc.scalar:
                nc.scalar.activation(dst, window.indirect(offsets), COPY)
            else:
                nc.vector.tensor_copy(dst, window.indirect(offsets))

        h = [sbuf("h" + str(t), [P, S], F32) for t in range(NT)]
        pa = [sbuf("pa" + str(t), [P, W], F32) for t in range(NT)]
        pb = [sbuf("pb" + str(t), [P, W], F32) for t in range(NT)]
        ra = [sbuf("ra" + str(t), [P, W], F32) for t in range(NT)]
        z_pairs = sbuf("z_pairs", [P, 2 * S * 2], BF16)
        z_pair = [z_pairs[:, 2 * S * u : 2 * S * (u + 1)].rearrange("p (j e) -> p j e", e=2) for u in range(2)]

        def h_out(t):
            nc.scalar.copy(h[t][:], h_ps[t][:])

        def h_fetch(t, engine):
            fetch(engine, pa[t][:], h[t][:], n1_t[:])
            fetch(engine, pb[t][:], h[t][:], n2_t[:])

        def h_max(t):
            nc.vector.tensor_tensor(ra[t][:], pa[t][:], pb[t][:], ALU.max)

        def h_put(t, engine):
            if engine is nc.scalar:
                nc.scalar.activation(h[t][:].indirect(n1_t[:]), ra[t][:], COPY)
            else:
                nc.vector.tensor_copy(h[t][:].indirect(n1_t[:]), ra[t][:])

        def z_round(t):
            engine = nc.gpsimd if t < 2 else nc.vector
            engine.tensor_scalar(
                z_pair[t // 2][:, :, t % 2], h[t][:], gain[:, t : t + 1], 0.0, ALU.mult, ALU.add
            )

        def deal_bytes(name, src):
            dst = sbuf(name, [P, S], U8)
            nc.vector.tensor_copy(
                dst[:].bitcast(I32).rearrange("p (t a w) -> p t a w", t=NT, w=2),
                src[:].bitcast(I32).rearrange("p (a t w) -> p t a w", t=NT, w=2),
            )
            return dst

        k2_b = gather_codes("k2_b", d_sc[:], k2_t, U8)
        w2_sc = deal_bytes("w2_sc", k2_b)
        lift_odd_rows(w2_sc, nc.sync)
        k2_w = gather_codes("k2_w", d_w32, k2_t, U32)
        w2_w = sbuf("w2_w", [P, S], U32)
        nc.vector.tensor_copy(
            w2_w[:].rearrange("p (t a b) -> p t a b", t=NT, b=8),
            k2_w[:].rearrange("p (a t b) -> p t a b", t=NT, b=8),
        )
        for t in range(2):
            h_out(t)
            h_fetch(t, nc.scalar)
            h_max(t)
        x2_w = gather_codes("x2_w", x_w32, two_t, U32)
        x2_sc = gather_codes("x2_sc", x_sc[:], two_t, U8)
        b_ps = [product("b", t, w2_w, w2_sc, x2_w, x2_sc) for t in range(NT)]
        h_out(2)
        h_out(3)
        fetch(nc.scalar, pa[3][:], h[3][:], n1_t[:])
        fetch(nc.vector, pb[3][:], h[3][:], n2_t[:])
        h_max(3)
        h_fetch(2, nc.scalar)
        h_max(2)
        for t in range(3):
            h_put(t, nc.scalar)
        h_put(3, nc.vector)
        xc_w = sbuf("xc_w", [P, S], U32, tag="pa0")
        nc.vector.tensor_copy(
            xc_w[:].rearrange("p (t a b) -> p a t b", t=NT, b=8), x_w32.indirect(cand_t[:])
        )
        xc_b = gather_codes("xc_b", x_sc[:], cand_t, U8, tag="pa1")
        xc_sc = deal_bytes("xc_sc", xc_b)
        for t in (0, 3, 1, 2):
            z_round(t)

        z = sbuf("z", [P, S * 4], BF16)
        z_w = sbuf("z_w", [P, S], U32)
        z_sc = sbuf("z_sc", [P, S], U8)
        halves = [slice(HALF * u, HALF * u + HALF) for u in range(2)]
        for cols in halves:
            nc.vector.tensor_copy(
                z[:].bitcast(F32).rearrange("p (j u) -> p j u", u=2)[:, cols, :],
                z_pairs[:].bitcast(F32).rearrange("p (u j) -> p j u", u=2)[:, cols, :],
            )
        for cols in halves:
            nc.vector.quantize_mx(
                out=z_w[:, cols].bitcast(FP8X4),
                scales=z_sc[:, cols],
                in_=z[:, 4 * cols.start : 4 * cols.stop],
            )
        a_ps = []
        for t in range(NT):
            bank = psum.tile([P, S], F32, name="ha" + str(t), tag="ha" + str(t))
            rows = slice(P * t, P * t + P)
            for cols in halves:
                nc.tensor.matmul_mx(
                    out=bank[:, cols],
                    lhsT=xc_w[:, rows].bitcast(FP8X4),
                    lhsT_scale=xc_sc[:, rows],
                    rhs=z_w[:, cols].bitcast(FP8X4),
                    rhs_scale=z_sc[:, cols],
                    start=True,
                    stop=True,
                )
            a_ps.append(bank)

        def tiles(name):
            return [sbuf(name + str(t), [P, S], F32) for t in range(NT)]

        a3, a4, b5 = tiles("a3"), tiles("a4"), tiles("b5")
        a_sb = {}
        d3, d4, first, second, res = tiles("d3"), tiles("d4"), tiles("first"), tiles("second"), tiles("res")
        b_sb = {}

        def fetch8(engine, dst, window, offsets):
            fetch(engine, dst[:], window[:], offsets[:])

        def b_out(t, engine, tag):
            b_sb[t] = sbuf("b_sb" + str(t), [P, 2 * S], F32, tag)
            if engine is nc.scalar:
                nc.scalar.activation(b_sb[t][:, 0:S], b_ps[t][:], COPY, scale=0.5 * 0.0625 * 0.0625)
            else:
                nc.vector.tensor_scalar(b_sb[t][:, 0:S], b_ps[t][:], 0.5 * 0.0625 * 0.0625, None, ALU.mult)

        def a_out(t, engine, tag):
            a_sb[t] = sbuf("a_sb" + str(t), [P, 2 * S], F32, tag)
            if engine is nc.scalar:
                nc.scalar.copy(a_sb[t][:, 0:S], a_ps[t][:])
            else:
                nc.vector.tensor_copy(a_sb[t][:, 0:S], a_ps[t][:])

        out_rows = out.rearrange("(a t b) j -> t a b j", t=NT, b=8)

        def first_term(t):
            nc.vector.tensor_tensor(d3[t][:], a3[t][:], a_ps[t][:], ALU.subtract)
            nc.vector.scalar_tensor_tensor(
                first[t][:], d3[t][:], 0.0625 * 0.0625, b_ps[t][:], ALU.mult, ALU.mult
            )

        def difference(t):
            if t == 0:
                nc.gpsimd.tensor_tensor(d4[t][:], a4[t][:], a_sb[t][:, 0:S], ALU.subtract)
            else:
                nc.vector.tensor_tensor(d4[t][:], a4[t][:], a_ps[t][:], ALU.subtract)

        def second_term(t, cols, engine):
            engine.tensor_tensor(second[t][:, cols], d4[t][:, cols], b5[t][:, cols], ALU.mult)

        def finish(t, cols, engine):
            engine.tensor_tensor(res[t][:, cols], first[t][:, cols], second[t][:, cols], ALU.add)
            nc.sync.dma_start(out_rows[t][:, :, cols], res[t][:, cols])

        def a_fetch(t):
            fetch8(nc.scalar, a4[t], a_sb[t], n4_t)
            fetch8(nc.scalar, a3[t], a_sb[t], n3_t)

        whole = slice(0, S)
        b_out(0, nc.scalar, "ra1")
        fetch8(nc.scalar, b5[0], b_sb[0], n5_t)
        b_out(1, nc.scalar, "ra2")
        a_out(0, nc.scalar, None)
        fetch8(nc.vector, b5[1], b_sb[1], n5_t)
        a_out(1, nc.vector, None)
        b_out(2, nc.vector, "z_pairs")
        fetch8(nc.vector, b5[2], b_sb[2], n5_t)
        a_out(2, nc.vector, None)
        for t in range(NT - 1):
            a_fetch(t)
            difference(t)
            second_term(t, whole, nc.gpsimd)
            first_term(t)
            finish(t, whole, nc.gpsimd)
            if t == 0:
                a_out(3, nc.vector, "a30")
            if t == 1:
                b_out(3, nc.vector, "a31")
        a_fetch(3)
        for u in range(2):
            fetch(nc.scalar, b5[3][:, halves[u]], b_sb[3][:], n5_t[:, 16 * u : 16 * u + 16])
        difference(3)
        first_term(3)
        for cols in halves:
            second_term(3, cols, nc.vector)
            finish(3, cols, nc.vector)
